import numpy as np
import ml_dtypes


def mxq(x, axis, fmt="e4m3"):
    dtype, down = {"e4m3": (ml_dtypes.float8_e4m3fn, 7), "e5m2": (ml_dtypes.float8_e5m2, 14)}[fmt]
    v = np.moveaxis(np.asarray(x, np.float32).astype(ml_dtypes.bfloat16).astype(np.float64), axis, -1)
    blocks = v.reshape(v.shape[:-1] + (-1, 32))
    amax = np.abs(blocks).max(-1, keepdims=True)
    byte = np.maximum(np.where(amax > 0, np.frexp(amax)[1] - 1 + 127, 0) - down, 1)
    scale = np.exp2(byte - 127.0)
    codes = (blocks / scale).astype(np.float32).astype(dtype).astype(np.float64)
    return np.moveaxis((codes * scale).reshape(v.shape), -1, axis)


WIDE = False


def mx_kscale(k):
    if not WIDE:
        return np.ones(k)
    levels = np.array([10, -10, 5, -5, 0])
    if k % 512:
        return np.exp2(np.random.permutation(np.resize(levels, k // 32))).repeat(32)
    a = np.empty((k // 512, 16))
    for p in range(k // 512):
        a[p, :8] = np.random.permutation(np.resize(levels, 8))
        for g in range(8):
            far = levels[np.abs(levels - a[p, g]) >= 10]
            a[p, g + 8] = far[np.random.randint(len(far))]
    return np.exp2(a.ravel()).repeat(32)


def f64(x):
    return np.asarray(x).astype(np.float64)


def striped(idx):
    return np.tile(idx.reshape(-1, 16).T, (8, 1)).astype(np.uint16)


def unstriped(offs):
    return offs[:16].T.reshape(-1).astype(np.int64)


def striped8(idx):
    return np.concatenate([x.reshape(-1, 16).T for x in idx]).astype(np.uint16)


def runs(offs, k):
    lists = np.stack([offs[16 * r : 16 * r + 16].T.reshape(-1) for r in range(8)]).astype(np.int64)
    return lists[np.arange(k) % 512 // 64]


def pack_weight(w):
    k, n = w.shape
    w = f64(np.asarray(w, np.float32).astype(ml_dtypes.bfloat16)).reshape(k // 32, 32, n)
    amax = np.abs(w).max(1)
    byte = np.clip(np.where(amax > 0, np.frexp(amax)[1] - 1 + 127 - 7, 1), 1, 254)
    scaled = (w * np.exp2(127.0 - byte)[:, None, :]).reshape(k, n).astype(np.float32)
    words = np.ascontiguousarray(scaled.reshape(k // 512, 128, 4, n).transpose(0, 1, 3, 2)).astype(ml_dtypes.float8_e4m3fn).view(np.uint8)
    return words, np.ascontiguousarray(byte.astype(np.uint8).reshape(k // 512, 16, n))


def unpack_weight(words, scales):
    g, p, n, _ = words.shape
    vals = np.ascontiguousarray(words).view(ml_dtypes.float8_e4m3fn).astype(np.float64) * np.repeat(np.exp2(scales.astype(np.float64) - 127.0), 8, axis=1)[..., None]
    return vals.transpose(0, 1, 3, 2).reshape(g * 512, n)


K, T, S, N, H, W = 512, 2048, 512, 512, 512, 384


def setup_inputs():
    n = np.random.standard_normal
    s = mx_kscale(K)[:, None]
    u = mx_kscale(H)
    packed_xT = pack_weight(n((K, T)) * s)
    return {
        "x_words": packed_xT[0],
        "x_scales": packed_xT[1],
        "w1": (n((K, H)) / np.sqrt(K) / s).astype(np.float32),
        "gn": (np.random.uniform(0.5, 1.5, (H, 1)) * u[:, None]).astype(np.float32),
        "w2": (n((H, N)) / np.sqrt(H) / u[:, None]).astype(np.float32),
        "offs": striped8(np.random.randint(0, T, (8, S))),
        "n1": striped(np.random.permutation(S)),
        "n2": striped(np.random.permutation(S)),
        "n3": striped(np.random.permutation(S)[:W]),
        "n4": striped(np.random.permutation(S)[:W]),
    }


def reference(x_words, x_scales, w1, gn, w2, offs, n1, n2, n3, n4):
    xq = unpack_weight(x_words, x_scales)[np.arange(K)[:, None], runs(offs, K)]
    y = mxq(f64(w1), 0, "e4m3").T @ xq
    st = y - y[:, unstriped(n1)]
    z = f64(gn) * (st / (np.abs(st[:, unstriped(n2)]) + 0.5))
    h = mxq(f64(w2), 0, "e4m3").T @ mxq(z, 0, "e4m3")
    old = h[:, unstriped(n3)]
    pa = h[:, unstriped(n4)]
    ra = old - (0.5 * pa)
    out = h.copy()
    out[:, unstriped(n3)] = ra
    return out

@@ -1,0 +1,230 @@
+from contextlib import ExitStack
+
+import concourse.mybir as mybir
+
+K, T, S, N, H, W = 512, 2048, 512, 512, 512, 384
+FLOPS = 2 * K * H * S + 2 * H * N * S
+
+F32 = mybir.dt.float32
+BF16 = mybir.dt.bfloat16
+I32 = mybir.dt.int32
+U32 = mybir.dt.uint32
+U16 = mybir.dt.uint16
+U8 = mybir.dt.uint8
+FP8X4 = mybir.dt.float8_e4m3fn_x4
+ALU = mybir.AluOpType
+ACT = mybir.ActivationFunctionType
+
+P = 128
+PACK = 4
+SPARE = 8
+HALF = S // 2
+CHUNKS = ((0, 256), (256, 384), (384, 512))
+M_SPLIT = 80
+
+
+def tile_picked_hashhopnkdif_none_p_kernel(
+    tc, x_words, x_scales, w1, gn, w2, offs, n1, n2, n3, n4, out
+):
+    nc = tc.nc
+    with ExitStack() as ctx:
+        keep = ctx.enter_context(tc.tile_pool(name="keep", bufs=1))
+        psum = ctx.enter_context(tc.psum_pool(name="psum", bufs=1))
+
+        offs_t = keep.tile([P, S // 16], U16, name="offs_t")
+        n1_t = keep.tile([P, S // 16], U16, name="n1_t")
+        n2_t = keep.tile([P, S // 16], U16, name="n2_t")
+        n3_t = keep.tile([P, W // 16], U16, name="n3_t")
+        n4_t = keep.tile([P, W // 16], U16, name="n4_t")
+
+        tab_bytes = keep.tile([P, T], U8, name="tab_bytes", align_bytes=64)
+        nc.gpsimd.memset(tab_bytes[:].bitcast(I32), 0)
+        for odd in range(2):
+            nc.gpsimd.dma_start(
+                out=tab_bytes[odd:P:16, :].bitcast(I32), in_=x_scales[0, odd:16:2, :].bitcast(I32)
+            )
+        gain = keep.tile([P, PACK], F32, name="gain")
+        nc.gpsimd.dma_start(out=gain[:], in_=gn.rearrange("(p t) o -> p (t o)", t=PACK))
+
+        nc.sync.dma_start(offs_t[:], offs)
+        w1_raw = keep.tile([P, PACK, H], F32, name="w1_raw")
+        w1_rows = w1.rearrange("(p j) c -> p j c", j=PACK)
+        for j in (0, 2):
+            nc.sync.dma_start(out=w1_raw[:, j : j + 2, :], in_=w1_rows[:, j : j + 2, :])
+        tab_words = keep.tile([P, T], U32, name="tab_words", align_bytes=64)
+        nc.sync.dma_start(
+            out=tab_words[:].bitcast(I32), in_=x_words[0].rearrange("p c r -> p (c r)").bitcast(I32)
+        )
+        nc.sync.dma_start(n1_t[:], n1)
+        nc.sync.dma_start(n2_t[:], n2)
+        nc.sync.dma_start(n3_t[:], n3)
+        nc.sync.dma_start(n4_t[:], n4)
+
+        half = keep.tile([P, 1], F32, name="half")
+        nc.vector.memset(half[:], 0.5)
+        y = [keep.tile([P, S + SPARE], F32, name="y%d" % t) for t in range(PACK)]
+        for t in range(PACK):
+            nc.vector.memset(y[t][:, S:], 0.0)
+
+        got_bytes = keep.tile([P, S], U8, name="got_bytes", tag="staged", align_bytes=64)
+        nc.vector.tensor_copy(got_bytes[:], tab_bytes[:].indirect(offs_t[:]))
+        x_scale = keep.tile([P, S], U8, name="x_scale", align_bytes=64)
+        nc.vector.tensor_copy(x_scale[:].bitcast(I32), got_bytes[:].bitcast(I32))
+        for r in range(2):
+            nc.scalar.dma_start(
+                out=x_scale[2 + r : P : 32, :].bitcast(I32), in_=got_bytes[16 + r : P : 32, :].bitcast(I32)
+            )
+
+        w1_bf = keep.tile([P, PACK, P, PACK], BF16, name="w1_bf", align_bytes=64)
+        w1_src = w1_raw[:].rearrange("p j (m t) -> p m j t", t=PACK)
+        w1_dst = w1_bf[:].rearrange("p t m j -> p m j t")
+        nc.vector.tensor_copy(out=w1_dst[:, :M_SPLIT], in_=w1_src[:, :M_SPLIT])
+        nc.scalar.copy(out=w1_dst[:, M_SPLIT:], in_=w1_src[:, M_SPLIT:])
+        w1_codes = keep.tile([P, H], U32, name="w1_codes", align_bytes=64)
+        w1_scale = keep.tile([P, H], U8, name="w1_scale", align_bytes=64)
+        nc.vector.quantize_mx(
+            out=w1_codes[:].bitcast(FP8X4), scales=w1_scale[:], in_=w1_bf[:].rearrange("p t m j -> p (t m j)")
+        )
+
+        w2_raw = keep.tile([P, PACK, N], F32, name="w2_raw", tag="staged", align_bytes=64)
+        nc.sync.dma_start(out=w2_raw[:], in_=w2.rearrange("(p j) c -> p j c", j=PACK))
+
+        x_codes = []
+        for u in range(2):
+            x_codes.append(keep.tile([P, HALF], U32, name="x_codes%d" % u, align_bytes=64))
+            nc.vector.tensor_copy(x_codes[u][:], tab_words[:].indirect(offs_t[:, 16 * u : 16 * (u + 1)]))
+
+        def first_product(t, u):
+            cols = slice(P * t, P * (t + 1))
+            places = slice(HALF * u, HALF * (u + 1))
+            acc = psum.tile([P, HALF], F32, name="y_acc%d_%d" % (t, u), tag="bank%d" % (4 * u + t))
+            nc.tensor.matmul_mx(
+                out=acc[:],
+                lhsT=w1_codes[:, cols].bitcast(FP8X4),
+                lhsT_scale=w1_scale[:, cols],
+                rhs=x_codes[u][:].bitcast(FP8X4),
+                rhs_scale=x_scale[:, places],
+                start=True,
+                stop=True,
+            )
+            if 2 * t + u < 3:
+                nc.scalar.copy(out=y[t][:, places], in_=acc[:])
+            else:
+                nc.vector.tensor_copy(out=y[t][:, places], in_=acc[:])
+
+        st = keep.tile([P, PACK, S], F32, name="st")
+        size = [keep.tile([P, S], F32, name="size%d" % t) for t in range(PACK)]
+
+        def difference(t):
+            y_at = keep.tile([P, S], F32, name="y_at%d" % t)
+            nc.scalar.activation(y_at[:], y[t][:].indirect(n1_t[:]), ACT.Copy)
+            nc.vector.tensor_tensor(st[:, t, :], y[t][:, :S], y_at[:], ALU.subtract)
+
+        def magnitude(t):
+            nc.vector.scalar_tensor_tensor(size[t][:], st[:, t, :], -1.0, st[:, t, :], ALU.mult, ALU.max)
+
+        w2_codes = [keep.tile([P, P], U32, name="w2_codes%d" % m, align_bytes=64) for m in range(N // P)]
+        w2_scale = [keep.tile([P, P], U8, name="w2_scale%d" % m, align_bytes=64) for m in range(N // P)]
+
+        def round_w2(m, tag):
+            w2_bf = keep.tile([P, P, PACK], BF16, name="w2_bf%d" % m, tag=tag, align_bytes=64)
+            nc.vector.tensor_copy(
+                out=w2_bf[:].rearrange("p (c i) j -> p c j i", i=4),
+                in_=w2_raw[:, :, P * m : P * (m + 1)].rearrange("p j (c i) -> p c j i", i=4),
+            )
+            return w2_bf
+
+        def quantise_w2(m, w2_bf):
+            nc.vector.quantize_mx(
+                out=w2_codes[m][:].bitcast(FP8X4), scales=w2_scale[m][:], in_=w2_bf[:].rearrange("p c j -> p (c j)")
+            )
+
+        for t in range(PACK - 1):
+            first_product(t, 0)
+            first_product(t, 1)
+        difference(0)
+        first_product(3, 0)
+        magnitude(0)
+        difference(1)
+        first_product(3, 1)
+        magnitude(1)
+        difference(2)
+        w2_first = round_w2(0, "w2_bf0")
+        magnitude(2)
+        difference(3)
+        quantise_w2(0, w2_first)
+        magnitude(3)
+
+        factor = []
+        for t in range(PACK):
+            root = keep.tile([P, S], F32, name="root%d" % t)
+            nc.scalar.activation(root[:], size[t][:], ACT.Abs_reciprocal_sqrt, bias=half[:])
+            factor.append(keep.tile([P, S], F32, name="factor%d" % t))
+            nc.vector.scalar_tensor_tensor(factor[t][:], root[:], gain[:, t : t + 1], root[:], ALU.mult, ALU.mult)
+
+        quantise_w2(1, round_w2(1, "w2_bf1"))
+
+        z_codes, z_scale = [], []
+        for n, (a, b) in enumerate(CHUNKS):
+            factor_at = keep.tile([P, PACK, b - a], F32, name="factor_at%d" % n)
+            for t in range(PACK):
+                nc.scalar.activation(factor_at[:, t, :], factor[t][:].indirect(n2_t[:, a // 16 : b // 16]), ACT.Copy)
+            z_bf = keep.tile([P, b - a, PACK], BF16, name="z_bf%d" % n, tag="z_bf%d" % n, align_bytes=64)
+            nc.vector.tensor_tensor(
+                z_bf[:].rearrange("p (c i) t -> p c t i", i=4),
+                st[:, :, a:b].rearrange("p t (c i) -> p c t i", i=4),
+                factor_at[:].rearrange("p t (c i) -> p c t i", i=4),
+                ALU.mult,
+            )
+            z_codes.append(keep.tile([P, b - a], U32, name="z_codes%d" % n, align_bytes=64))
+            z_scale.append(keep.tile([P, b - a], U8, name="z_scale%d" % n, align_bytes=64))
+            nc.vector.quantize_mx(
+                out=z_codes[n][:].bitcast(FP8X4), scales=z_scale[n][:], in_=z_bf[:].rearrange("p c t -> p (c t)")
+            )
+
+        last = CHUNKS[-1][0]
+        h = [keep.tile([P, S], F32, name="h%d" % m) for m in range(N // P)]
+        mix = [keep.tile([P, W], F32, name="mix%d" % m) for m in range(N // P)]
+
+        def second_product(m):
+            early = psum.tile([P, last], F32, name="h_early%d" % m, tag="bank%d" % (4 + m))
+            late = psum.tile([P, S - last], F32, name="h_late%d" % m, tag="bank%d" % m)
+            for n, (a, b) in enumerate(CHUNKS):
+                nc.tensor.matmul_mx(
+                    out=early[:, a:b] if a < last else late[:],
+                    lhsT=w2_codes[m][:].bitcast(FP8X4),
+                    lhsT_scale=w2_scale[m][:],
+                    rhs=z_codes[n][:].bitcast(FP8X4),
+                    rhs_scale=z_scale[n][:],
+                    start=True,
+                    stop=True,
+                )
+            if m < 2:
+                nc.scalar.copy(out=h[m][:, :last], in_=early[:])
+            else:
+                nc.vector.tensor_copy(out=h[m][:, :last], in_=early[:])
+            if m < 1:
+                nc.scalar.copy(out=h[m][:, last:], in_=late[:])
+            else:
+                nc.vector.tensor_copy(out=h[m][:, last:], in_=late[:])
+
+        def look_up(m):
+            old = keep.tile([P, W], F32, name="old%d" % m)
+            nc.scalar.activation(old[:], h[m][:].indirect(n3_t[:]), ACT.Copy, scale=-2.0)
+            nc.vector.tensor_tensor(mix[m][:], h[m][:].indirect(n4_t[:]), old[:], ALU.add)
+
+        def put_back(m):
+            nc.scalar.activation(h[m][:].indirect(n3_t[:]), mix[m][:], ACT.Copy, scale=-0.5)
+            nc.sync.dma_start(out=out[P * m : P * (m + 1), :], in_=h[m][:])
+
+        second_product(0)
+        second_product(1)
+        look_up(0)
+        look_up(1)
+        put_back(0)
+        for m in range(2, N // P):
+            quantise_w2(m, round_w2(m, "z_bf%d" % (len(CHUNKS) - 1)))
+            second_product(m)
+            look_up(m)
+            put_back(m - 1)
+        put_back(N // P - 1)

@@ -37,42 +37,40 @@ def tile_picked_hashhopnkdif_none_p_kernel(
         n3_t = keep.tile([P, W // 16], U16, name="n3_t")
         n4_t = keep.tile([P, W // 16], U16, name="n4_t")
 
-        tab_bytes = keep.tile([P, T], U8, name="tab_bytes", align_bytes=64)
-        nc.gpsimd.memset(tab_bytes[:].bitcast(I32), 0)
-        for odd in range(2):
-            nc.gpsimd.dma_start(
-                out=tab_bytes[odd:P:16, :].bitcast(I32), in_=x_scales[0, odd:16:2, :].bitcast(I32)
-            )
+        tab_bytes = keep.tile([P, T], U8, name="tab_bytes", tag="staged0", align_bytes=64)
+        nc.sync.dma_start(
+            out=tab_bytes[:].bitcast(I32), in_=x_scales[0].bitcast(I32).unsqueeze(1).to_broadcast([16, 8, T // 4])
+        )
         gain = keep.tile([P, PACK], F32, name="gain")
-        nc.gpsimd.dma_start(out=gain[:], in_=gn.rearrange("(p t) o -> p (t o)", t=PACK))
+        nc.scalar.dma_start(out=gain[:], in_=gn.rearrange("(p t) o -> p (t o)", t=PACK))
 
         nc.sync.dma_start(offs_t[:], offs)
+        nc.sync.dma_start(n1_t[:], n1)
+        nc.sync.dma_start(n2_t[:], n2)
         w1_raw = keep.tile([P, PACK, H], F32, name="w1_raw")
-        w1_rows = w1.rearrange("(p j) c -> p j c", j=PACK)
-        for j in (0, 2):
-            nc.sync.dma_start(out=w1_raw[:, j : j + 2, :], in_=w1_rows[:, j : j + 2, :])
+        nc.sync.dma_start(out=w1_raw[:], in_=w1.rearrange("(p j) c -> p j c", j=PACK))
         tab_words = keep.tile([P, T], U32, name="tab_words", align_bytes=64)
         nc.sync.dma_start(
             out=tab_words[:].bitcast(I32), in_=x_words[0].rearrange("p c r -> p (c r)").bitcast(I32)
         )
-        nc.sync.dma_start(n1_t[:], n1)
-        nc.sync.dma_start(n2_t[:], n2)
         nc.sync.dma_start(n3_t[:], n3)
         nc.sync.dma_start(n4_t[:], n4)
 
         half = keep.tile([P, 1], F32, name="half")
         nc.vector.memset(half[:], 0.5)
+        warm = keep.tile([P, 1], F32, name="warm")
+        nc.scalar.activation(warm[:], half[:], ACT.Abs_reciprocal_sqrt, bias=half[:])
         y = [keep.tile([P, S + SPARE], F32, name="y%d" % t) for t in range(PACK)]
         for t in range(PACK):
             nc.vector.memset(y[t][:, S:], 0.0)
 
-        got_bytes = keep.tile([P, S], U8, name="got_bytes", tag="staged", align_bytes=64)
+        got_bytes = keep.tile([P, S], U8, name="got_bytes", tag="staged1", align_bytes=64)
         nc.vector.tensor_copy(got_bytes[:], tab_bytes[:].indirect(offs_t[:]))
         x_scale = keep.tile([P, S], U8, name="x_scale", align_bytes=64)
-        nc.vector.tensor_copy(x_scale[:].bitcast(I32), got_bytes[:].bitcast(I32))
-        for r in range(2):
+        nc.vector.memset(x_scale[:].bitcast(I32), 0)
+        for r in range(4):
             nc.scalar.dma_start(
-                out=x_scale[2 + r : P : 32, :].bitcast(I32), in_=got_bytes[16 + r : P : 32, :].bitcast(I32)
+                out=x_scale[r:P:32, :].bitcast(I32), in_=got_bytes[8 * r : P : 32, :].bitcast(I32)
             )
 
         w1_bf = keep.tile([P, PACK, P, PACK], BF16, name="w1_bf", align_bytes=64)
@@ -86,8 +84,11 @@ def tile_picked_hashhopnkdif_none_p_kernel(
             out=w1_codes[:].bitcast(FP8X4), scales=w1_scale[:], in_=w1_bf[:].rearrange("p t m j -> p (t m j)")
         )
 
-        w2_raw = keep.tile([P, PACK, N], F32, name="w2_raw", tag="staged", align_bytes=64)
-        nc.sync.dma_start(out=w2_raw[:], in_=w2.rearrange("(p j) c -> p j c", j=PACK))
+        w2_rows = w2.rearrange("(p j) c -> p j c", j=PACK)
+        w2_raw = []
+        for u in range(2):
+            w2_raw.append(keep.tile([P, PACK, N // 2], F32, name="w2_raw%d" % u, tag="staged%d" % u, align_bytes=64))
+            nc.sync.dma_start(out=w2_raw[u][:], in_=w2_rows[:, :, N // 2 * u : N // 2 * (u + 1)])
 
         x_codes = []
         for u in range(2):
@@ -107,7 +108,7 @@ def tile_picked_hashhopnkdif_none_p_kernel(
                 start=True,
                 stop=True,
             )
-            if 2 * t + u < 3:
+            if t == 0:
                 nc.scalar.copy(out=y[t][:, places], in_=acc[:])
             else:
                 nc.vector.tensor_copy(out=y[t][:, places], in_=acc[:])
@@ -123,57 +124,46 @@ def tile_picked_hashhopnkdif_none_p_kernel(
         def magnitude(t):
             nc.vector.scalar_tensor_tensor(size[t][:], st[:, t, :], -1.0, st[:, t, :], ALU.mult, ALU.max)
 
-        w2_codes = [keep.tile([P, P], U32, name="w2_codes%d" % m, align_bytes=64) for m in range(N // P)]
-        w2_scale = [keep.tile([P, P], U8, name="w2_scale%d" % m, align_bytes=64) for m in range(N // P)]
+        w2_codes = keep.tile([P, N], U32, name="w2_codes", align_bytes=64)
+        w2_scale = keep.tile([P, N], U8, name="w2_scale", align_bytes=64)
 
-        def round_w2(m, tag):
-            w2_bf = keep.tile([P, P, PACK], BF16, name="w2_bf%d" % m, tag=tag, align_bytes=64)
-            nc.vector.tensor_copy(
-                out=w2_bf[:].rearrange("p (c i) j -> p c j i", i=4),
-                in_=w2_raw[:, :, P * m : P * (m + 1)].rearrange("p j (c i) -> p c j i", i=4),
-            )
-            return w2_bf
-
-        def quantise_w2(m, w2_bf):
+        def quantise_w2(cols, w2_bf):
             nc.vector.quantize_mx(
-                out=w2_codes[m][:].bitcast(FP8X4), scales=w2_scale[m][:], in_=w2_bf[:].rearrange("p c j -> p (c j)")
+                out=w2_codes[:, cols].bitcast(FP8X4), scales=w2_scale[:, cols], in_=w2_bf[:].rearrange("p c j -> p (c j)")
             )
 
-        for t in range(PACK - 1):
+        w2_early = keep.tile([P, N // 2, PACK], BF16, name="w2_early", align_bytes=64)
+        nc.gpsimd.tensor_scalar(w2_early[:], w2_raw[0][:].rearrange("p j c -> p c j"), 1.0, 0.0, ALU.mult, ALU.add)
+
+        for t in range(PACK):
             first_product(t, 0)
             first_product(t, 1)
-        difference(0)
-        first_product(3, 0)
-        magnitude(0)
-        difference(1)
-        first_product(3, 1)
-        magnitude(1)
-        difference(2)
-        w2_first = round_w2(0, "w2_bf0")
-        magnitude(2)
-        difference(3)
-        quantise_w2(0, w2_first)
-        magnitude(3)
+        for t in range(PACK):
+            difference(t)
+            magnitude(t)
 
         factor = []
         for t in range(PACK):
-            root = keep.tile([P, S], F32, name="root%d" % t)
+            root = keep.tile([P, S], F32, name="root%d" % t, tag="root%d" % t)
             nc.scalar.activation(root[:], size[t][:], ACT.Abs_reciprocal_sqrt, bias=half[:])
             factor.append(keep.tile([P, S], F32, name="factor%d" % t))
             nc.vector.scalar_tensor_tensor(factor[t][:], root[:], gain[:, t : t + 1], root[:], ALU.mult, ALU.mult)
 
-        quantise_w2(1, round_w2(1, "w2_bf1"))
+        quantise_w2(slice(0, N // 2), w2_early)
+
+        first_at = keep.tile([P, PACK, HALF], F32, name="first_at")
+        later_at = keep.tile([P, 2, PACK, HALF // 2], F32, name="later_at", tag="root%d" % (PACK - 1))
 
         z_codes, z_scale = [], []
         for n, (a, b) in enumerate(CHUNKS):
-            factor_at = keep.tile([P, PACK, b - a], F32, name="factor_at%d" % n)
+            factor_at = first_at[:] if n == 0 else later_at[:, n - 1]
             for t in range(PACK):
                 nc.scalar.activation(factor_at[:, t, :], factor[t][:].indirect(n2_t[:, a // 16 : b // 16]), ACT.Copy)
             z_bf = keep.tile([P, b - a, PACK], BF16, name="z_bf%d" % n, tag="z_bf%d" % n, align_bytes=64)
             nc.vector.tensor_tensor(
                 z_bf[:].rearrange("p (c i) t -> p c t i", i=4),
                 st[:, :, a:b].rearrange("p t (c i) -> p c t i", i=4),
-                factor_at[:].rearrange("p t (c i) -> p c t i", i=4),
+                factor_at.rearrange("p t (c i) -> p c t i", i=4),
                 ALU.mult,
             )
             z_codes.append(keep.tile([P, b - a], U32, name="z_codes%d" % n, align_bytes=64))
@@ -192,8 +182,8 @@ def tile_picked_hashhopnkdif_none_p_kernel(
             for n, (a, b) in enumerate(CHUNKS):
                 nc.tensor.matmul_mx(
                     out=early[:, a:b] if a < last else late[:],
-                    lhsT=w2_codes[m][:].bitcast(FP8X4),
-                    lhsT_scale=w2_scale[m][:],
+                    lhsT=w2_codes[:, P * m : P * (m + 1)].bitcast(FP8X4),
+                    lhsT_scale=w2_scale[:, P * m : P * (m + 1)],
                     rhs=z_codes[n][:].bitcast(FP8X4),
                     rhs_scale=z_scale[n][:],
                     start=True,
@@ -210,11 +200,13 @@ def tile_picked_hashhopnkdif_none_p_kernel(
 
         def look_up(m):
             old = keep.tile([P, W], F32, name="old%d" % m)
-            nc.scalar.activation(old[:], h[m][:].indirect(n3_t[:]), ACT.Copy, scale=-2.0)
-            nc.vector.tensor_tensor(mix[m][:], h[m][:].indirect(n4_t[:]), old[:], ALU.add)
+            nc.scalar.activation(old[:], h[m][:].indirect(n3_t[:]), ACT.Copy)
+            pa = keep.tile([P, W], F32, name="pa%d" % m)
+            nc.vector.tensor_copy(pa[:], h[m][:].indirect(n4_t[:]))
+            nc.vector.scalar_tensor_tensor(mix[m][:], pa[:], -0.5, old[:], ALU.mult, ALU.add)
 
         def put_back(m):
-            nc.scalar.activation(h[m][:].indirect(n3_t[:]), mix[m][:], ACT.Copy, scale=-0.5)
+            nc.scalar.activation(h[m][:].indirect(n3_t[:]), mix[m][:], ACT.Copy)
             nc.sync.dma_start(out=out[P * m : P * (m + 1), :], in_=h[m][:])
 
         second_product(0)
@@ -223,7 +215,12 @@ def tile_picked_hashhopnkdif_none_p_kernel(
         look_up(1)
         put_back(0)
         for m in range(2, N // P):
-            quantise_w2(m, round_w2(m, "z_bf%d" % (len(CHUNKS) - 1)))
+            w2_late = keep.tile([P, P, PACK], BF16, name="w2_late%d" % m, tag="z_bf%d" % (len(CHUNKS) - 1), align_bytes=64)
+            nc.vector.tensor_copy(
+                out=w2_late[:].rearrange("p (c i) j -> p c j i", i=4),
+                in_=w2_raw[1][:, :, P * (m - 2) : P * (m - 1)].rearrange("p j (c i) -> p c j i", i=4),
+            )
+            quantise_w2(slice(P * m, P * (m + 1)), w2_late)
             second_product(m)
             look_up(m)
             put_back(m - 1)

@@ -124,7 +124,6 @@ def tile_picked_hashhopnkdif_none_p_kernel(
         def magnitude(t):
             nc.vector.scalar_tensor_tensor(size[t][:], st[:, t, :], -1.0, st[:, t, :], ALU.mult, ALU.max)
 
-        w2_codes = keep.tile([P, N], U32, name="w2_codes", align_bytes=64)
         w2_scale = keep.tile([P, N], U8, name="w2_scale", align_bytes=64)
 
         def quantise_w2(cols, w2_bf):
@@ -144,33 +143,50 @@ def tile_picked_hashhopnkdif_none_p_kernel(
 
         factor = []
         for t in range(PACK):
-            root = keep.tile([P, S], F32, name="root%d" % t, tag="root%d" % t)
+            root = keep.tile([P, S], F32, name="root%d" % t, tag="root%d" % t, align_bytes=64)
             nc.scalar.activation(root[:], size[t][:], ACT.Abs_reciprocal_sqrt, bias=half[:])
             factor.append(keep.tile([P, S], F32, name="factor%d" % t))
             nc.vector.scalar_tensor_tensor(factor[t][:], root[:], gain[:, t : t + 1], root[:], ALU.mult, ALU.mult)
 
+        w2_codes = keep.tile([P, N], U32, name="w2_codes", tag="root%d" % (PACK - 2), align_bytes=64)
         quantise_w2(slice(0, N // 2), w2_early)
 
         first_at = keep.tile([P, PACK, HALF], F32, name="first_at")
-        later_at = keep.tile([P, 2, PACK, HALF // 2], F32, name="later_at", tag="root%d" % (PACK - 1))
+        later_at = keep.tile([P, 2, PACK, HALF // 2], F32, name="later_at", tag="root%d" % (PACK - 1), align_bytes=64)
 
-        z_codes, z_scale = [], []
-        for n, (a, b) in enumerate(CHUNKS):
+        z_bf, z_codes, z_scale = [], [], []
+
+        def normalise(n):
+            a, b = CHUNKS[n]
             factor_at = first_at[:] if n == 0 else later_at[:, n - 1]
             for t in range(PACK):
-                nc.scalar.activation(factor_at[:, t, :], factor[t][:].indirect(n2_t[:, a // 16 : b // 16]), ACT.Copy)
-            z_bf = keep.tile([P, b - a, PACK], BF16, name="z_bf%d" % n, tag="z_bf%d" % n, align_bytes=64)
+                looked_up = factor[t][:].indirect(n2_t[:, a // 16 : b // 16])
+                if n == 0 and t == PACK - 1:
+                    nc.vector.tensor_copy(factor_at[:, t, :], looked_up)
+                else:
+                    nc.scalar.activation(factor_at[:, t, :], looked_up, ACT.Copy)
+            z_bf.append(keep.tile([P, b - a, PACK], BF16, name="z_bf%d" % n, tag="z_bf%d" % n, align_bytes=64))
             nc.vector.tensor_tensor(
-                z_bf[:].rearrange("p (c i) t -> p c t i", i=4),
+                z_bf[n][:].rearrange("p (c i) t -> p c t i", i=4),
                 st[:, :, a:b].rearrange("p t (c i) -> p c t i", i=4),
                 factor_at.rearrange("p t (c i) -> p c t i", i=4),
                 ALU.mult,
             )
+
+        def quantise_z(n):
+            a, b = CHUNKS[n]
             z_codes.append(keep.tile([P, b - a], U32, name="z_codes%d" % n, align_bytes=64))
             z_scale.append(keep.tile([P, b - a], U8, name="z_scale%d" % n, align_bytes=64))
             nc.vector.quantize_mx(
-                out=z_codes[n][:].bitcast(FP8X4), scales=z_scale[n][:], in_=z_bf[:].rearrange("p c t -> p (c t)")
+                out=z_codes[n][:].bitcast(FP8X4), scales=z_scale[n][:], in_=z_bf[n][:].rearrange("p c t -> p (c t)")
             )
+
+        normalise(0)
+        normalise(1)
+        quantise_z(0)
+        quantise_z(1)
+        normalise(2)
+        quantise_z(2)
 
         last = CHUNKS[-1][0]
         h = [keep.tile([P, S], F32, name="h%d" % m) for m in range(N // P)]
@@ -198,23 +214,15 @@ def tile_picked_hashhopnkdif_none_p_kernel(
             else:
                 nc.vector.tensor_copy(out=h[m][:, last:], in_=late[:])
 
-        def look_up(m):
-            old = keep.tile([P, W], F32, name="old%d" % m)
-            nc.scalar.activation(old[:], h[m][:].indirect(n3_t[:]), ACT.Copy)
-            pa = keep.tile([P, W], F32, name="pa%d" % m)
-            nc.vector.tensor_copy(pa[:], h[m][:].indirect(n4_t[:]))
-            nc.vector.scalar_tensor_tensor(mix[m][:], pa[:], -0.5, old[:], ALU.mult, ALU.add)
+        old = [keep.tile([P, W], F32, name="old%d" % m) for m in range(N // P)]
 
-        def put_back(m):
-            nc.scalar.activation(h[m][:].indirect(n3_t[:]), mix[m][:], ACT.Copy)
-            nc.sync.dma_start(out=out[P * m : P * (m + 1), :], in_=h[m][:])
+        def fetch_old(m):
+            nc.scalar.activation(old[m][:], h[m][:].indirect(n3_t[:]), ACT.Copy, scale=-2.0)
 
         second_product(0)
         second_product(1)
-        look_up(0)
-        look_up(1)
-        put_back(0)
         for m in range(2, N // P):
+            fetch_old(m - 2)
             w2_late = keep.tile([P, P, PACK], BF16, name="w2_late%d" % m, tag="z_bf%d" % (len(CHUNKS) - 1), align_bytes=64)
             nc.vector.tensor_copy(
                 out=w2_late[:].rearrange("p (c i) j -> p c j i", i=4),
@@ -222,6 +230,9 @@ def tile_picked_hashhopnkdif_none_p_kernel(
             )
             quantise_w2(slice(P * m, P * (m + 1)), w2_late)
             second_product(m)
-            look_up(m)
-            put_back(m - 1)
-        put_back(N // P - 1)
+        for m in range(2, N // P):
+            fetch_old(m)
+        for m in range(N // P):
+            nc.vector.tensor_tensor(mix[m][:], h[m][:].indirect(n4_t[:]), old[m][:], ALU.add)
+            nc.scalar.activation(h[m][:].indirect(n3_t[:]), mix[m][:], ACT.Copy, scale=-0.5)
+            nc.sync.dma_start(out=out[P * m : P * (m + 1), :], in_=h[m][:])

@@ -41,18 +41,16 @@ def tile_picked_hashhopnkdif_none_p_kernel(
         nc.sync.dma_start(
             out=tab_bytes[:].bitcast(I32), in_=x_scales[0].bitcast(I32).unsqueeze(1).to_broadcast([16, 8, T // 4])
         )
-        gain = keep.tile([P, PACK], F32, name="gain")
-        nc.scalar.dma_start(out=gain[:], in_=gn.rearrange("(p t) o -> p (t o)", t=PACK))
 
         nc.sync.dma_start(offs_t[:], offs)
         nc.sync.dma_start(n1_t[:], n1)
-        nc.sync.dma_start(n2_t[:], n2)
-        w1_raw = keep.tile([P, PACK, H], F32, name="w1_raw")
+        w1_raw = keep.tile([P, PACK, H], F32, name="w1_raw", tag="staged2", align_bytes=64)
         nc.sync.dma_start(out=w1_raw[:], in_=w1.rearrange("(p j) c -> p j c", j=PACK))
         tab_words = keep.tile([P, T], U32, name="tab_words", align_bytes=64)
         nc.sync.dma_start(
             out=tab_words[:].bitcast(I32), in_=x_words[0].rearrange("p c r -> p (c r)").bitcast(I32)
         )
+        nc.sync.dma_start(n2_t[:], n2)
         nc.sync.dma_start(n3_t[:], n3)
         nc.sync.dma_start(n4_t[:], n4)
 
@@ -67,8 +65,8 @@ def tile_picked_hashhopnkdif_none_p_kernel(
         got_bytes = keep.tile([P, S], U8, name="got_bytes", tag="staged1", align_bytes=64)
         nc.vector.tensor_copy(got_bytes[:], tab_bytes[:].indirect(offs_t[:]))
         x_scale = keep.tile([P, S], U8, name="x_scale", align_bytes=64)
-        nc.vector.memset(x_scale[:].bitcast(I32), 0)
-        for r in range(4):
+        nc.vector.tensor_copy(x_scale[:].bitcast(I32), got_bytes[:].bitcast(I32))
+        for r in range(1, 4):
             nc.scalar.dma_start(
                 out=x_scale[r:P:32, :].bitcast(I32), in_=got_bytes[8 * r : P : 32, :].bitcast(I32)
             )
@@ -89,6 +87,9 @@ def tile_picked_hashhopnkdif_none_p_kernel(
         for u in range(2):
             w2_raw.append(keep.tile([P, PACK, N // 2], F32, name="w2_raw%d" % u, tag="staged%d" % u, align_bytes=64))
             nc.sync.dma_start(out=w2_raw[u][:], in_=w2_rows[:, :, N // 2 * u : N // 2 * (u + 1)])
+
+        gain = keep.tile([P, PACK], F32, name="gain", tag="staged2", align_bytes=64)
+        nc.sync.dma_start(out=gain[:], in_=gn.rearrange("(p t) o -> p (t o)", t=PACK))
 
         x_codes = []
         for u in range(2):

from contextlib import ExitStack

import concourse.mybir as mybir

K, T, S, N, H, W = 512, 2048, 512, 512, 512, 384
FLOPS = 2 * K * H * S + 2 * H * N * S

F32 = mybir.dt.float32
BF16 = mybir.dt.bfloat16
I32 = mybir.dt.int32
U32 = mybir.dt.uint32
U16 = mybir.dt.uint16
U8 = mybir.dt.uint8
FP8X4 = mybir.dt.float8_e4m3fn_x4
ALU = mybir.AluOpType
ACT = mybir.ActivationFunctionType

P = 128
PACK = 4
SPARE = 8
HALF = S // 2
CHUNKS = ((0, 256), (256, 384), (384, 512))
M_SPLIT = 80


def tile_picked_hashhopnkdif_none_p_kernel(
    tc, x_words, x_scales, w1, gn, w2, offs, n1, n2, n3, n4, out
):
    nc = tc.nc
    with ExitStack() as ctx:
        keep = ctx.enter_context(tc.tile_pool(name="keep", bufs=1))
        psum = ctx.enter_context(tc.psum_pool(name="psum", bufs=1))

        offs_t = keep.tile([P, S // 16], U16, name="offs_t")
        n1_t = keep.tile([P, S // 16], U16, name="n1_t")
        n2_t = keep.tile([P, S // 16], U16, name="n2_t")
        n3_t = keep.tile([P, W // 16], U16, name="n3_t")
        n4_t = keep.tile([P, W // 16], U16, name="n4_t")

        tab_bytes = keep.tile([P, T], U8, name="tab_bytes", tag="staged0", align_bytes=64)
        nc.sync.dma_start(
            out=tab_bytes[:].bitcast(I32), in_=x_scales[0].bitcast(I32).unsqueeze(1).to_broadcast([16, 8, T // 4])
        )

        nc.sync.dma_start(offs_t[:], offs)
        nc.sync.dma_start(n1_t[:], n1)
        w1_raw = keep.tile([P, PACK, H], F32, name="w1_raw", tag="staged2", align_bytes=64)
        nc.sync.dma_start(out=w1_raw[:], in_=w1.rearrange("(p j) c -> p j c", j=PACK))
        tab_words = keep.tile([P, T], U32, name="tab_words", align_bytes=64)
        nc.sync.dma_start(
            out=tab_words[:].bitcast(I32), in_=x_words[0].rearrange("p c r -> p (c r)").bitcast(I32)
        )
        nc.sync.dma_start(n2_t[:], n2)
        nc.sync.dma_start(n3_t[:], n3)
        nc.sync.dma_start(n4_t[:], n4)

        half = keep.tile([P, 1], F32, name="half")
        nc.vector.memset(half[:], 0.5)
        warm = keep.tile([P, 1], F32, name="warm")
        nc.scalar.activation(warm[:], half[:], ACT.Abs_reciprocal_sqrt, bias=half[:])
        y = [keep.tile([P, S + SPARE], F32, name="y%d" % t) for t in range(PACK)]
        for t in range(PACK):
            nc.vector.memset(y[t][:, S:], 0.0)

        got_bytes = keep.tile([P, S], U8, name="got_bytes", tag="staged1", align_bytes=64)
        nc.vector.tensor_copy(got_bytes[:], tab_bytes[:].indirect(offs_t[:]))
        x_scale = keep.tile([P, S], U8, name="x_scale", align_bytes=64)
        nc.vector.tensor_copy(x_scale[:].bitcast(I32), got_bytes[:].bitcast(I32))
        for r in range(1, 4):
            nc.scalar.dma_start(
                out=x_scale[r:P:32, :].bitcast(I32), in_=got_bytes[8 * r : P : 32, :].bitcast(I32)
            )

        w1_bf = keep.tile([P, PACK, P, PACK], BF16, name="w1_bf", align_bytes=64)
        w1_src = w1_raw[:].rearrange("p j (m t) -> p m j t", t=PACK)
        w1_dst = w1_bf[:].rearrange("p t m j -> p m j t")
        nc.vector.tensor_copy(out=w1_dst[:, :M_SPLIT], in_=w1_src[:, :M_SPLIT])
        nc.scalar.copy(out=w1_dst[:, M_SPLIT:], in_=w1_src[:, M_SPLIT:])
        w1_codes = keep.tile([P, H], U32, name="w1_codes", align_bytes=64)
        w1_scale = keep.tile([P, H], U8, name="w1_scale", align_bytes=64)
        nc.vector.quantize_mx(
            out=w1_codes[:].bitcast(FP8X4), scales=w1_scale[:], in_=w1_bf[:].rearrange("p t m j -> p (t m j)")
        )

        w2_rows = w2.rearrange("(p j) c -> p j c", j=PACK)
        w2_raw = []
        for u in range(2):
            w2_raw.append(keep.tile([P, PACK, N // 2], F32, name="w2_raw%d" % u, tag="staged%d" % u, align_bytes=64))
            nc.sync.dma_start(out=w2_raw[u][:], in_=w2_rows[:, :, N // 2 * u : N // 2 * (u + 1)])

        gain = keep.tile([P, PACK], F32, name="gain", tag="staged2", align_bytes=64)
        nc.sync.dma_start(out=gain[:], in_=gn.rearrange("(p t) o -> p (t o)", t=PACK))

        x_codes = []
        for u in range(2):
            x_codes.append(keep.tile([P, HALF], U32, name="x_codes%d" % u, align_bytes=64))
            nc.vector.tensor_copy(x_codes[u][:], tab_words[:].indirect(offs_t[:, 16 * u : 16 * (u + 1)]))

        def first_product(t, u):
            cols = slice(P * t, P * (t + 1))
            places = slice(HALF * u, HALF * (u + 1))
            acc = psum.tile([P, HALF], F32, name="y_acc%d_%d" % (t, u), tag="bank%d" % (4 * u + t))
            nc.tensor.matmul_mx(
                out=acc[:],
                lhsT=w1_codes[:, cols].bitcast(FP8X4),
                lhsT_scale=w1_scale[:, cols],
                rhs=x_codes[u][:].bitcast(FP8X4),
                rhs_scale=x_scale[:, places],
                start=True,
                stop=True,
            )
            if t == 0:
                nc.scalar.copy(out=y[t][:, places], in_=acc[:])
            else:
                nc.vector.tensor_copy(out=y[t][:, places], in_=acc[:])

        st = keep.tile([P, PACK, S], F32, name="st")
        size = [keep.tile([P, S], F32, name="size%d" % t) for t in range(PACK)]

        def difference(t):
            y_at = keep.tile([P, S], F32, name="y_at%d" % t)
            nc.scalar.activation(y_at[:], y[t][:].indirect(n1_t[:]), ACT.Copy)
            nc.vector.tensor_tensor(st[:, t, :], y[t][:, :S], y_at[:], ALU.subtract)

        def magnitude(t):
            nc.vector.scalar_tensor_tensor(size[t][:], st[:, t, :], -1.0, st[:, t, :], ALU.mult, ALU.max)

        w2_scale = keep.tile([P, N], U8, name="w2_scale", align_bytes=64)

        def quantise_w2(cols, w2_bf):
            nc.vector.quantize_mx(
                out=w2_codes[:, cols].bitcast(FP8X4), scales=w2_scale[:, cols], in_=w2_bf[:].rearrange("p c j -> p (c j)")
            )

        w2_early = keep.tile([P, N // 2, PACK], BF16, name="w2_early", align_bytes=64)
        nc.gpsimd.tensor_scalar(w2_early[:], w2_raw[0][:].rearrange("p j c -> p c j"), 1.0, 0.0, ALU.mult, ALU.add)

        for t in range(PACK):
            first_product(t, 0)
            first_product(t, 1)
        for t in range(PACK):
            difference(t)
            magnitude(t)

        factor = []
        for t in range(PACK):
            root = keep.tile([P, S], F32, name="root%d" % t, tag="root%d" % t, align_bytes=64)
            nc.scalar.activation(root[:], size[t][:], ACT.Abs_reciprocal_sqrt, bias=half[:])
            factor.append(keep.tile([P, S], F32, name="factor%d" % t))
            nc.vector.scalar_tensor_tensor(factor[t][:], root[:], gain[:, t : t + 1], root[:], ALU.mult, ALU.mult)

        w2_codes = keep.tile([P, N], U32, name="w2_codes", tag="root%d" % (PACK - 2), align_bytes=64)
        quantise_w2(slice(0, N // 2), w2_early)

        first_at = keep.tile([P, PACK, HALF], F32, name="first_at")
        later_at = keep.tile([P, 2, PACK, HALF // 2], F32, name="later_at", tag="root%d" % (PACK - 1), align_bytes=64)

        z_bf, z_codes, z_scale = [], [], []

        def normalise(n):
            a, b = CHUNKS[n]
            factor_at = first_at[:] if n == 0 else later_at[:, n - 1]
            for t in range(PACK):
                looked_up = factor[t][:].indirect(n2_t[:, a // 16 : b // 16])
                if n == 0 and t == PACK - 1:
                    nc.vector.tensor_copy(factor_at[:, t, :], looked_up)
                else:
                    nc.scalar.activation(factor_at[:, t, :], looked_up, ACT.Copy)
            z_bf.append(keep.tile([P, b - a, PACK], BF16, name="z_bf%d" % n, tag="z_bf%d" % n, align_bytes=64))
            nc.vector.tensor_tensor(
                z_bf[n][:].rearrange("p (c i) t -> p c t i", i=4),
                st[:, :, a:b].rearrange("p t (c i) -> p c t i", i=4),
                factor_at.rearrange("p t (c i) -> p c t i", i=4),
                ALU.mult,
            )

        def quantise_z(n):
            a, b = CHUNKS[n]
            z_codes.append(keep.tile([P, b - a], U32, name="z_codes%d" % n, align_bytes=64))
            z_scale.append(keep.tile([P, b - a], U8, name="z_scale%d" % n, align_bytes=64))
            nc.vector.quantize_mx(
                out=z_codes[n][:].bitcast(FP8X4), scales=z_scale[n][:], in_=z_bf[n][:].rearrange("p c t -> p (c t)")
            )

        normalise(0)
        normalise(1)
        quantise_z(0)
        quantise_z(1)
        normalise(2)
        quantise_z(2)

        last = CHUNKS[-1][0]
        h = [keep.tile([P, S], F32, name="h%d" % m) for m in range(N // P)]
        mix = [keep.tile([P, W], F32, name="mix%d" % m) for m in range(N // P)]

        def second_product(m):
            early = psum.tile([P, last], F32, name="h_early%d" % m, tag="bank%d" % (4 + m))
            late = psum.tile([P, S - last], F32, name="h_late%d" % m, tag="bank%d" % m)
            for n, (a, b) in enumerate(CHUNKS):
                nc.tensor.matmul_mx(
                    out=early[:, a:b] if a < last else late[:],
                    lhsT=w2_codes[:, P * m : P * (m + 1)].bitcast(FP8X4),
                    lhsT_scale=w2_scale[:, P * m : P * (m + 1)],
                    rhs=z_codes[n][:].bitcast(FP8X4),
                    rhs_scale=z_scale[n][:],
                    start=True,
                    stop=True,
                )
            if m < 2:
                nc.scalar.copy(out=h[m][:, :last], in_=early[:])
            else:
                nc.vector.tensor_copy(out=h[m][:, :last], in_=early[:])
            if m < 1:
                nc.scalar.copy(out=h[m][:, last:], in_=late[:])
            else:
                nc.vector.tensor_copy(out=h[m][:, last:], in_=late[:])

        old = [keep.tile([P, W], F32, name="old%d" % m) for m in range(N // P)]

        def fetch_old(m):
            nc.scalar.activation(old[m][:], h[m][:].indirect(n3_t[:]), ACT.Copy, scale=-2.0)

        second_product(0)
        second_product(1)
        for m in range(2, N // P):
            fetch_old(m - 2)
            w2_late = keep.tile([P, P, PACK], BF16, name="w2_late%d" % m, tag="z_bf%d" % (len(CHUNKS) - 1), align_bytes=64)
            nc.vector.tensor_copy(
                out=w2_late[:].rearrange("p (c i) j -> p c j i", i=4),
                in_=w2_raw[1][:, :, P * (m - 2) : P * (m - 1)].rearrange("p j (c i) -> p c j i", i=4),
            )
            quantise_w2(slice(P * m, P * (m + 1)), w2_late)
            second_product(m)
        for m in range(2, N // P):
            fetch_old(m)
        for m in range(N // P):
            nc.vector.tensor_tensor(mix[m][:], h[m][:].indirect(n4_t[:]), old[m][:], ALU.add)
            nc.scalar.activation(h[m][:].indirect(n3_t[:]), mix[m][:], ACT.Copy, scale=-0.5)
            nc.sync.dma_start(out=out[P * m : P * (m + 1), :], in_=h[m][:])
